import numpy as np
import ml_dtypes


def mxq(x, axis, fmt="e4m3"):
    dtype, down = {"e4m3": (ml_dtypes.float8_e4m3fn, 7), "e5m2": (ml_dtypes.float8_e5m2, 14)}[fmt]
    v = np.moveaxis(np.asarray(x, np.float32).astype(ml_dtypes.bfloat16).astype(np.float64), axis, -1)
    blocks = v.reshape(v.shape[:-1] + (-1, 32))
    amax = np.abs(blocks).max(-1, keepdims=True)
    byte = np.maximum(np.where(amax > 0, np.frexp(amax)[1] - 1 + 127, 0) - down, 1)
    scale = np.exp2(byte - 127.0)
    codes = (blocks / scale).astype(np.float32).astype(dtype).astype(np.float64)
    return np.moveaxis((codes * scale).reshape(v.shape), -1, axis)


WIDE = False


def mx_kscale(k):
    if not WIDE:
        return np.ones(k)
    levels = np.array([30, -30])
    if k % 512:
        return np.exp2(np.random.permutation(np.resize(levels, k // 32))).repeat(32)
    a = np.empty((k // 512, 16))
    for p in range(k // 512):
        a[p, :8] = np.random.permutation(np.resize(levels, 8))
        for g in range(8):
            far = levels[np.abs(levels - a[p, g]) >= 10]
            a[p, g + 8] = far[np.random.randint(len(far))]
    return np.exp2(a.ravel()).repeat(32)


def f64(x):
    return np.asarray(x).astype(np.float64)


def striped(idx):
    return np.tile(np.asarray(idx).reshape(-1, 16).T, (8, 1)).astype(np.uint16)


def unstriped(offs):
    return offs[:16].T.reshape(-1).astype(np.int64)


def striped8(idx):
    return np.asarray(idx).reshape(8, -1, 16).transpose(0, 2, 1).reshape(128, -1).astype(np.uint16)


def unstriped8(offs):
    return offs.reshape(8, 16, -1).transpose(0, 2, 1).reshape(8, -1).astype(np.int64)


def pick8(x, idx, run):
    r = np.arange(len(x))
    return x[r[:, None], idx[r % (8 * run) // run]]


E2M1 = np.array([0.0, 0.5, 1.0, 1.5, 2.0, 3.0, 4.0, 6.0, -0.0, -0.5, -1.0, -1.5, -2.0, -3.0, -4.0, -6.0])


def pack_weight(w, fmt):
    k, n = w.shape
    w = f64(np.asarray(w, np.float32).astype(ml_dtypes.bfloat16)).reshape(k // 32, 32, n)
    amax = np.abs(w).max(1)
    if fmt in ("e4m3", "e5m2"):
        byte = np.frexp(amax)[1] - 1 + 127 - (7 if fmt == "e4m3" else 14)
    else:
        mant, ex = np.frexp(amax / 6.0)
        byte = np.where(mant > 0.5, ex, ex - 1) + 127
    byte = np.clip(np.where(amax > 0, byte, 1), 1, 254)
    scaled = (w * np.exp2(127.0 - byte)[:, None, :]).reshape(k, n).astype(np.float32)
    by_word = np.ascontiguousarray(scaled.reshape(k // 512, 128, 4, n).transpose(0, 1, 3, 2))
    if fmt in ("e4m3", "e5m2"):
        words = by_word.astype(ml_dtypes.float8_e4m3fn if fmt == "e4m3" else ml_dtypes.float8_e5m2).view(np.uint8)
    else:
        c = by_word.astype(ml_dtypes.float4_e2m1fn).view(np.uint8) & 0xF
        words = (c[..., 0::2] | (c[..., 1::2] << 4)).reshape(k // 512, 128, 2 * n)
    return np.ascontiguousarray(words), np.ascontiguousarray(byte.astype(np.uint8).reshape(k // 512, 16, n))


def unpack_weight(words, scales, fmt):
    g, _, n = scales.shape
    words = np.ascontiguousarray(words).reshape(g, 128, n, -1)
    if fmt in ("e4m3", "e5m2"):
        vals = words.view(ml_dtypes.float8_e4m3fn if fmt == "e4m3" else ml_dtypes.float8_e5m2).astype(np.float64)
    else:
        nib = np.empty((g, 128, n, 4), np.uint8)
        nib[..., 0::2] = words & 0xF
        nib[..., 1::2] = words >> 4
        vals = E2M1[nib]
    vals = vals * np.repeat(np.exp2(scales.astype(np.float64) - 127.0), 8, axis=1)[..., None]
    return vals.transpose(0, 1, 3, 2).reshape(g * 512, n)


def sigmoid(v):
    return 1.0 / (1.0 + np.exp(-v))


def sgn(shape):
    return np.random.uniform(0.5, 2.0, shape) * np.where(np.random.standard_normal(shape) < 0, -1.0, 1.0)


K, T, J, R, F, Z, N, O = 512, 1024, 256, 512, 512, 1024, 256, 128


def setup_inputs():
    n = np.random.standard_normal
    idx = np.random.permutation(T)[:J]
    idx2 = np.random.permutation(Z)[:J]
    idx3 = np.stack([np.random.permutation(J)[:O] for _ in range(8)])
    idx4 = np.stack([np.random.permutation(J)[:O] for _ in range(8)])
    idx5 = np.random.permutation(J)[:O]
    fk = mx_kscale(K)
    ff = mx_kscale(F)
    fr = mx_kscale(R)
    xtp = pack_weight(n((K, T)) / fk[:, None], "e5m2")
    xop = pack_weight(n((F, Z)) / ff[:, None], "e4m3")
    wp = pack_weight(n((K, R)) * 1 / np.sqrt(K) * fk[:, None] * fr, "e2m1")
    w0p = pack_weight(n((F, R)) * 1 / np.sqrt(F) * ff[:, None] * fr, "e2m1")
    w2p = pack_weight(n((F, R)) * 1 / np.sqrt(F) * ff[:, None] * fr, "e4m3")
    wbp = pack_weight(n((R, N)) * 1 / np.sqrt(R) / fr[:, None], "e2m1")
    wcp = pack_weight(n((R, N)) * 1 / np.sqrt(R) / fr[:, None], "e4m3")
    return {
        "xt_words": xtp[0],
        "xt_scales": xtp[1],
        "xo_words": xop[0],
        "xo_scales": xop[1],
        "w_words": wp[0],
        "w_scales": wp[1],
        "w0_words": w0p[0],
        "w0_scales": w0p[1],
        "w2_words": w2p[0],
        "w2_scales": w2p[1],
        "wb_words": wbp[0],
        "wb_scales": wbp[1],
        "wc_words": wcp[0],
        "wc_scales": wcp[1],
        "so": (np.random.uniform(0.5, 1.6, (N, 1))).astype(np.float32),
        "sp": (sgn((N, 1))).astype(np.float32),
        "bo": (np.random.uniform(-2.0, 2.0, (N, 1))).astype(np.float32),
        "offs": striped(idx),
        "offs2": striped(idx2),
        "offs3": striped8(idx3),
        "offs4": striped8(idx4),
        "offs5": striped(idx5),
    }


def reference(xt_words, xt_scales, xo_words, xo_scales, w_words, w_scales, w0_words, w0_scales, w2_words, w2_scales, wb_words, wb_scales, wc_words, wc_scales, so, sp, bo, offs, offs2, offs3, offs4, offs5):
    idx = unstriped(offs)
    idx2 = unstriped(offs2)
    idx3 = unstriped8(offs3)
    idx4 = unstriped8(offs4)
    idx5 = unstriped(offs5)
    xtu = unpack_weight(xt_words, xt_scales, "e5m2")
    xou = unpack_weight(xo_words, xo_scales, "e4m3")
    wu = unpack_weight(w_words, w_scales, "e2m1")
    w0u = unpack_weight(w0_words, w0_scales, "e2m1")
    w2u = unpack_weight(w2_words, w2_scales, "e4m3")
    wbu = unpack_weight(wb_words, wb_scales, "e2m1")
    wcu = unpack_weight(wc_words, wc_scales, "e4m3")
    xtidxg = xtu[:, idx]
    xoidx2g = xou[:, idx2]
    a = wu.T @ xtidxg + w0u.T @ xoidx2g
    b = w2u.T @ xoidx2g
    hid = np.abs(a - b)
    hidq = mxq(hid, 0, "e4m3")
    p = wbu.T @ hidq
    q = wcu.T @ hidq
    y = pick8(p, idx3, 16) * f64(so) * sigmoid(pick8(p, idx4, 16) * f64(sp) + f64(bo)) - q[:, idx5]
    return y

@@ -1,0 +1,207 @@
+from contextlib import ExitStack
+
+import concourse.mybir as mybir
+from concourse.masks import make_identity
+
+K, T, J, R, N, O = 512, 1024, 256, 512, 256, 128
+FLOPS = 3 * 2 * K * R * J + 2 * 2 * R * N * J
+
+F32 = mybir.dt.float32
+BF16 = mybir.dt.bfloat16
+I32 = mybir.dt.int32
+U32 = mybir.dt.uint32
+U16 = mybir.dt.uint16
+U8 = mybir.dt.uint8
+E4M3 = mybir.dt.float8_e4m3fn_x4
+E5M2 = mybir.dt.float8_e5m2_x4
+E2M1 = mybir.dt.float4_e2m1fn_x4
+ACT = mybir.ActivationFunctionType
+ALU = mybir.AluOpType
+
+P = 128
+HALF = 64
+
+
+def tile_list_outcomegatedgroups_noted_kernel(
+    tc, xt_words, xt_scales, xo_words, xo_scales, w_words, w_scales, w0_words, w0_scales,
+    w2_words, w2_scales, wb_words, wb_scales, wc_words, wc_scales, so, sp, bo,
+    offs, offs2, offs3, offs4, offs5, out,
+):
+    nc = tc.nc
+    with ExitStack() as ctx:
+        sb = ctx.enter_context(tc.tile_pool(name="sb", bufs=1))
+        ps = ctx.enter_context(tc.psum_pool(name="ps", bufs=1))
+
+        def load_list(src, name):
+            t = sb.tile(list(src.shape), U16, name=name)
+            nc.sync.dma_start(t[:], src)
+            return t
+
+        def load_words(src, name):
+            flat = src[0]
+            if len(flat.shape) == 3:
+                flat = flat.rearrange("p n t -> p (n t)")
+            t = sb.tile([P, flat.shape[1]], U8, name=name, align_bytes=64)
+            nc.sync.dma_start(t[:].bitcast(I32), flat.bitcast(I32))
+            return t
+
+        def load_scale_rows(queue, src, stage, base, col0):
+            rows = src[0].bitcast(I32).rearrange("(s q r) n -> q r s n", s=2, q=2)
+            width = rows.shape[3]
+            for q in range(2):
+                p0 = base + 32 * q
+                queue.dma_start(stage[p0 : p0 + 4, :, col0 : col0 + width], rows[q])
+
+        xo_stage = sb.tile([P, 2, T // 4], I32, name="xo_stage", align_bytes=64)
+        xt_stage = sb.tile([P, 2, T // 4], I32, name="xt_stage", align_bytes=64)
+        w2_sc = sb.tile([P, 2, R // 4], I32, name="w2_sc", align_bytes=64)
+        w0_sc = sb.tile([P, 2, R // 4], I32, name="w0_sc", align_bytes=64)
+        w_sc = sb.tile([P, 2, R // 4], I32, name="w_sc", align_bytes=64)
+        wbc_sc = sb.tile([P, 2, 2 * N // 4], I32, name="wbc_sc", align_bytes=64)
+        nc.vector.memset(xo_stage[0:HALF], 0)
+        nc.vector.memset(w2_sc[0:HALF], 0)
+        nc.gpsimd.memset(w0_sc[HALF:P], 0)
+        nc.gpsimd.memset(w_sc[HALF:P], 0)
+        nc.vector.memset(xt_stage[HALF:P], 0)
+        nc.vector.memset(wbc_sc[0:HALF], 0)
+
+        l2 = load_list(offs2, "l2")
+        load_scale_rows(nc.sync, xo_scales, xo_stage, 0, 0)
+        load_scale_rows(nc.sync, w2_scales, w2_sc, 0, 0)
+        load_scale_rows(nc.gpsimd, w0_scales, w0_sc, HALF, 0)
+        xo_w = load_words(xo_words, "xo_w")
+        w2_w = load_words(w2_words, "w2_w")
+        w0_w = load_words(w0_words, "w0_w")
+        l1 = load_list(offs, "l1")
+        load_scale_rows(nc.sync, xt_scales, xt_stage, HALF, 0)
+        xt_w = load_words(xt_words, "xt_w")
+        w_w = load_words(w_words, "w_w")
+        load_scale_rows(nc.sync, w_scales, w_sc, HALF, 0)
+        load_scale_rows(nc.sync, wb_scales, wbc_sc, 0, 0)
+        load_scale_rows(nc.sync, wc_scales, wbc_sc, 0, N // 4)
+        wb_w = load_words(wb_words, "wb_w")
+        wc_w = load_words(wc_words, "wc_w")
+        l4 = load_list(offs4, "l4")
+        l3 = load_list(offs3, "l3")
+        l5 = load_list(offs5, "l5")
+        vecs = []
+        with nc.allow_non_contiguous_dma(reason="one value a partition and half"):
+            for src, name in ((sp, "sp_t"), (bo, "bo_t"), (so, "so_t")):
+                t = sb.tile([P, 2], F32, name=name)
+                nc.sync.dma_start(t[:], src.rearrange("(h p) o -> p (h o)", p=P))
+                vecs.append(t)
+        sp_t, bo_t, so_t = vecs
+
+        ident = sb.tile([P, P], F32, name="ident")
+        make_identity(nc, ident[:])
+
+        def plane_of(sc, base):
+            if base == 0:
+                nc.vector.tensor_copy(sc[HALF:P, 0, :], sc[0:HALF, 1, :])
+                return sc[:, 0, :].bitcast(U8)
+            nc.vector.tensor_copy(sc[0:HALF, 1, :], sc[HALF:P, 0, :])
+            return sc[:, 1, :].bitcast(U8)
+
+        def gathered_plane(stage, base, lst, name):
+            plane = sb.tile([P, T], U8, name=name + "_plane", align_bytes=64)
+            pv = plane[:].bitcast(I32)
+            nc.vector.tensor_copy(pv[0:HALF], stage[base : base + HALF, 0, :])
+            nc.vector.tensor_copy(pv[HALF:P], stage[base : base + HALF, 1, :])
+            g = sb.tile([P, J], U8, name=name + "_gs", align_bytes=64)
+            nc.vector.tensor_copy(g[:], plane[:].indirect(lst[:]))
+            return g
+
+        def gather_words(words, lst, jt, g):
+            nc.vector.tensor_copy(
+                g[:, jt * P : (jt + 1) * P],
+                words[:].bitcast(U32).indirect(lst[:, jt * 8 : (jt + 1) * 8]),
+            )
+
+        xo_gs = gathered_plane(xo_stage, 0, l2, "xo")
+        w2_pl = plane_of(w2_sc, 0)
+        xo_g = sb.tile([P, J], U32, name="xo_g", align_bytes=64)
+        xt_g = sb.tile([P, J], U32, name="xt_g", align_bytes=64)
+        b_ps = [ps.tile([P, R], F32, name=f"b{jt}", tag=f"bank{jt}") for jt in range(2)]
+        a_ps = [ps.tile([P, R], F32, name=f"a{jt}", tag=f"bank{2 + jt}") for jt in range(2)]
+        b_sb = [sb.tile([P, 4, P], F32, name=f"b_sb{jt}") for jt in range(2)]
+        for jt in range(2):
+            js = slice(jt * P, (jt + 1) * P)
+            gather_words(xo_w, l2, jt, xo_g)
+            nc.tensor.matmul_mx(
+                b_ps[jt][:], lhsT=xo_g[:, js].bitcast(E4M3), lhsT_scale=xo_gs[:, js],
+                rhs=w2_w[:].bitcast(E4M3), rhs_scale=w2_pl, start=True, stop=True,
+            )
+            nc.scalar.copy(b_sb[jt][:], b_ps[jt][:].rearrange("j (p t) -> j t p", t=4))
+        w0_pl = plane_of(w0_sc, HALF)
+        for jt in range(2):
+            js = slice(jt * P, (jt + 1) * P)
+            nc.tensor.matmul_mx(
+                a_ps[jt][:], lhsT=xo_g[:, js].bitcast(E4M3), lhsT_scale=xo_gs[:, js],
+                rhs=w0_w[:].bitcast(E2M1), rhs_scale=w0_pl, start=True, stop=False,
+            )
+        xt_gs = gathered_plane(xt_stage, HALF, l1, "xt")
+        w_pl = plane_of(w_sc, HALF)
+        for jt in range(2):
+            js = slice(jt * P, (jt + 1) * P)
+            gather_words(xt_w, l1, jt, xt_g)
+            nc.tensor.matmul_mx(
+                a_ps[jt][:], lhsT=xt_g[:, js].bitcast(E5M2), lhsT_scale=xt_gs[:, js],
+                rhs=w_w[:].bitcast(E2M1), rhs_scale=w_pl, start=False, stop=True,
+            )
+        wbc_pl = plane_of(wbc_sc, 0)
+
+        hid = []
+        for jt in range(2):
+            d = sb.tile([P, 4, P], F32, name=f"d{jt}")
+            nc.vector.tensor_tensor(
+                d[:], a_ps[jt][:].rearrange("j (p t) -> j t p", t=4), b_sb[jt][:], ALU.subtract
+            )
+            tr = ps.tile([P, 4, P], F32, name=f"tr{jt}", tag=f"bank{4 + jt}")
+            for t in range(4):
+                nc.tensor.transpose(tr[:, t, :], d[:, t, :], ident[:])
+            h = sb.tile([P, P, 4], BF16, name=f"hid{jt}", align_bytes=64)
+            nc.scalar.activation(h[:], tr[:].rearrange("p t j -> p j t"), ACT.Abs)
+            hid.append(h)
+
+        p_sb = [sb.tile([P, J], F32, name=f"p_sb{h}") for h in range(2)]
+        q_sb = sb.tile([P, 2, J], F32, name="q_sb")
+        for jt in range(2):
+            js = slice(jt * P, (jt + 1) * P)
+            codes = sb.tile([P, P], U32, name=f"codes{jt}", align_bytes=64)
+            hsc = sb.tile([P, P], U8, name=f"hsc{jt}", align_bytes=64)
+            nc.vector.quantize_mx(
+                out=codes[:].bitcast(E4M3), scales=hsc[:], in_=hid[jt][:].rearrange("p j t -> p (j t)")
+            )
+            p_ps = [ps.tile([P, P], F32, name=f"p{jt}{h}", tag=f"bank{(0, 1, 6, 7)[2 * jt + h]}") for h in range(2)]
+            q_ps = ps.tile([P, 2, P], F32, name=f"q{jt}", tag=f"bank{2 + jt}")
+            for h in range(2):
+                nc.tensor.matmul_mx(
+                    p_ps[h][:], lhsT=wb_w[:, 2 * P * h : 2 * P * (h + 1)].bitcast(E2M1),
+                    lhsT_scale=wbc_pl[:, P * h : P * (h + 1)],
+                    rhs=codes[:].bitcast(E4M3), rhs_scale=hsc[:], start=True, stop=True,
+                )
+            for h in range(2):
+                nc.tensor.matmul_mx(
+                    q_ps[:, h, :], lhsT=wc_w[:, 4 * P * h : 4 * P * (h + 1)].bitcast(E4M3),
+                    lhsT_scale=wbc_pl[:, N + P * h : N + P * (h + 1)],
+                    rhs=codes[:].bitcast(E4M3), rhs_scale=hsc[:], start=True, stop=True,
+                )
+            nc.scalar.copy(p_sb[0][:, js], p_ps[0][:])
+            nc.vector.tensor_copy(p_sb[1][:, js], p_ps[1][:])
+            nc.vector.tensor_copy(q_sb[:, :, js], q_ps[:])
+
+        for h in range(2):
+            gate = sb.tile([P, O], F32, name=f"gate{h}")
+            val = sb.tile([P, O], F32, name=f"val{h}")
+            qg = sb.tile([P, O], F32, name=f"qg{h}")
+            prod = sb.tile([P, O], F32, name=f"prod{h}")
+            res = sb.tile([P, O], F32, name=f"res{h}")
+            nc.scalar.activation(
+                gate[:], p_sb[h][:].indirect(l4[:]), ACT.Sigmoid,
+                bias=bo_t[:, h : h + 1], scale=sp_t[:, h : h + 1],
+            )
+            nc.scalar.activation(val[:], p_sb[h][:].indirect(l3[:]), ACT.Copy, scale=so_t[:, h : h + 1])
+            nc.vector.tensor_copy(qg[:], q_sb[:, h, :].indirect(l5[:]))
+            nc.vector.tensor_tensor(prod[:], val[:], gate[:], ALU.mult)
+            nc.vector.tensor_tensor(res[:], prod[:], qg[:], ALU.subtract)
+            nc.sync.dma_start(out[h * P : (h + 1) * P, :], res[:])

@@ -20,6 +20,7 @@ ALU = mybir.AluOpType
 
 P = 128
 HALF = 64
+W2_ROW = 4
 
 
 def tile_list_outcomegatedgroups_noted_kernel(
@@ -58,39 +59,41 @@ def tile_list_outcomegatedgroups_noted_kernel(
         w0_sc = sb.tile([P, 2, R // 4], I32, name="w0_sc", align_bytes=64)
         w_sc = sb.tile([P, 2, R // 4], I32, name="w_sc", align_bytes=64)
         wbc_sc = sb.tile([P, 2, 2 * N // 4], I32, name="wbc_sc", align_bytes=64)
-        nc.vector.memset(xo_stage[0:HALF], 0)
+        nc.gpsimd.memset(xo_stage[0:HALF], 0)
+        nc.vector.memset(w0_sc[HALF:P], 0)
         nc.vector.memset(w2_sc[0:HALF], 0)
-        nc.gpsimd.memset(w0_sc[HALF:P], 0)
-        nc.gpsimd.memset(w_sc[HALF:P], 0)
-        nc.vector.memset(xt_stage[HALF:P], 0)
+        nc.gpsimd.memset(xt_stage[HALF:P], 0)
+        nc.vector.memset(w_sc[0:HALF], 0)
         nc.vector.memset(wbc_sc[0:HALF], 0)
 
+        def load_vec(src, name):
+            t = sb.tile([P, 2], F32, name=name)
+            with nc.allow_non_contiguous_dma(reason="one value a partition and half"):
+                nc.sync.dma_start(t[:], src.rearrange("(h p) o -> p (h o)", p=P))
+            return t
+
         l2 = load_list(offs2, "l2")
-        load_scale_rows(nc.sync, xo_scales, xo_stage, 0, 0)
-        load_scale_rows(nc.sync, w2_scales, w2_sc, 0, 0)
-        load_scale_rows(nc.gpsimd, w0_scales, w0_sc, HALF, 0)
-        xo_w = load_words(xo_words, "xo_w")
-        w2_w = load_words(w2_words, "w2_w")
-        w0_w = load_words(w0_words, "w0_w")
         l1 = load_list(offs, "l1")
+        load_scale_rows(nc.sync, xo_scales, xo_stage, 0, 0)
+        load_scale_rows(nc.sync, w0_scales, w0_sc, HALF, 0)
+        xo_w = load_words(xo_words, "xo_w")
+        w0_w = load_words(w0_words, "w0_w")
+        load_scale_rows(nc.sync, w2_scales, w2_sc, W2_ROW, 0)
+        w2_w = load_words(w2_words, "w2_w")
         load_scale_rows(nc.sync, xt_scales, xt_stage, HALF, 0)
         xt_w = load_words(xt_words, "xt_w")
+        load_scale_rows(nc.sync, w_scales, w_sc, 0, 0)
         w_w = load_words(w_words, "w_w")
-        load_scale_rows(nc.sync, w_scales, w_sc, HALF, 0)
         load_scale_rows(nc.sync, wb_scales, wbc_sc, 0, 0)
         load_scale_rows(nc.sync, wc_scales, wbc_sc, 0, N // 4)
         wb_w = load_words(wb_words, "wb_w")
         wc_w = load_words(wc_words, "wc_w")
         l4 = load_list(offs4, "l4")
+        sp_t = load_vec(sp, "sp_t")
+        bo_t = load_vec(bo, "bo_t")
         l3 = load_list(offs3, "l3")
+        so_t = load_vec(so, "so_t")
         l5 = load_list(offs5, "l5")
-        vecs = []
-        with nc.allow_non_contiguous_dma(reason="one value a partition and half"):
-            for src, name in ((sp, "sp_t"), (bo, "bo_t"), (so, "so_t")):
-                t = sb.tile([P, 2], F32, name=name)
-                nc.sync.dma_start(t[:], src.rearrange("(h p) o -> p (h o)", p=P))
-                vecs.append(t)
-        sp_t, bo_t, so_t = vecs
 
         ident = sb.tile([P, P], F32, name="ident")
         make_identity(nc, ident[:])
@@ -102,48 +105,48 @@ def tile_list_outcomegatedgroups_noted_kernel(
             nc.vector.tensor_copy(sc[0:HALF, 1, :], sc[HALF:P, 0, :])
             return sc[:, 1, :].bitcast(U8)
 
-        def gathered_plane(stage, base, lst, name):
-            plane = sb.tile([P, T], U8, name=name + "_plane", align_bytes=64)
+        def table_plane(stage, base, name):
+            plane = sb.tile([P, T], U8, name=name, align_bytes=64)
             pv = plane[:].bitcast(I32)
             nc.vector.tensor_copy(pv[0:HALF], stage[base : base + HALF, 0, :])
             nc.vector.tensor_copy(pv[HALF:P], stage[base : base + HALF, 1, :])
-            g = sb.tile([P, J], U8, name=name + "_gs", align_bytes=64)
-            nc.vector.tensor_copy(g[:], plane[:].indirect(lst[:]))
-            return g
+            return plane
 
-        def gather_words(words, lst, jt, g):
-            nc.vector.tensor_copy(
-                g[:, jt * P : (jt + 1) * P],
-                words[:].bitcast(U32).indirect(lst[:, jt * 8 : (jt + 1) * 8]),
-            )
+        def gather(words, plane, lst, jt, g, gs):
+            js = slice(jt * P, (jt + 1) * P)
+            piece = lst[:, jt * 8 : (jt + 1) * 8]
+            nc.vector.tensor_copy(gs[:, js], plane[:].indirect(piece))
+            nc.vector.tensor_copy(g[:, js], words[:].bitcast(U32).indirect(piece))
 
-        xo_gs = gathered_plane(xo_stage, 0, l2, "xo")
-        w2_pl = plane_of(w2_sc, 0)
+        xo_pl = table_plane(xo_stage, 0, "xo_pl")
+        w0_pl = plane_of(w0_sc, HALF)
         xo_g = sb.tile([P, J], U32, name="xo_g", align_bytes=64)
         xt_g = sb.tile([P, J], U32, name="xt_g", align_bytes=64)
+        xo_gs = sb.tile([P, J], U8, name="xo_gs", align_bytes=64)
+        xt_gs = sb.tile([P, J], U8, name="xt_gs", align_bytes=64)
         b_ps = [ps.tile([P, R], F32, name=f"b{jt}", tag=f"bank{jt}") for jt in range(2)]
         a_ps = [ps.tile([P, R], F32, name=f"a{jt}", tag=f"bank{2 + jt}") for jt in range(2)]
         b_sb = [sb.tile([P, 4, P], F32, name=f"b_sb{jt}") for jt in range(2)]
         for jt in range(2):
             js = slice(jt * P, (jt + 1) * P)
-            gather_words(xo_w, l2, jt, xo_g)
+            gather(xo_w, xo_pl, l2, jt, xo_g, xo_gs)
+            nc.tensor.matmul_mx(
+                a_ps[jt][:], lhsT=xo_g[:, js].bitcast(E4M3), lhsT_scale=xo_gs[:, js],
+                rhs=w0_w[:].bitcast(E2M1), rhs_scale=w0_pl, start=True, stop=False,
+            )
+        w2_pl = plane_of(w2_sc, 0)[W2_ROW:P]
+        for jt in range(2):
+            js = slice(jt * P, (jt + 1) * P)
             nc.tensor.matmul_mx(
                 b_ps[jt][:], lhsT=xo_g[:, js].bitcast(E4M3), lhsT_scale=xo_gs[:, js],
                 rhs=w2_w[:].bitcast(E4M3), rhs_scale=w2_pl, start=True, stop=True,
             )
             nc.scalar.copy(b_sb[jt][:], b_ps[jt][:].rearrange("j (p t) -> j t p", t=4))
-        w0_pl = plane_of(w0_sc, HALF)
+        xt_pl = table_plane(xt_stage, HALF, "xt_pl")
+        w_pl = plane_of(w_sc, 0)
         for jt in range(2):
             js = slice(jt * P, (jt + 1) * P)
-            nc.tensor.matmul_mx(
-                a_ps[jt][:], lhsT=xo_g[:, js].bitcast(E4M3), lhsT_scale=xo_gs[:, js],
-                rhs=w0_w[:].bitcast(E2M1), rhs_scale=w0_pl, start=True, stop=False,
-            )
-        xt_gs = gathered_plane(xt_stage, HALF, l1, "xt")
-        w_pl = plane_of(w_sc, HALF)
-        for jt in range(2):
-            js = slice(jt * P, (jt + 1) * P)
-            gather_words(xt_w, l1, jt, xt_g)
+            gather(xt_w, xt_pl, l1, jt, xt_g, xt_gs)
             nc.tensor.matmul_mx(
                 a_ps[jt][:], lhsT=xt_g[:, js].bitcast(E5M2), lhsT_scale=xt_gs[:, js],
                 rhs=w_w[:].bitcast(E2M1), rhs_scale=w_pl, start=False, stop=True,
@@ -153,12 +156,13 @@ def tile_list_outcomegatedgroups_noted_kernel(
         hid = []
         for jt in range(2):
             d = sb.tile([P, 4, P], F32, name=f"d{jt}")
-            nc.vector.tensor_tensor(
-                d[:], a_ps[jt][:].rearrange("j (p t) -> j t p", t=4), b_sb[jt][:], ALU.subtract
-            )
             tr = ps.tile([P, 4, P], F32, name=f"tr{jt}", tag=f"bank{4 + jt}")
-            for t in range(4):
-                nc.tensor.transpose(tr[:, t, :], d[:, t, :], ident[:])
+            a_v = a_ps[jt][:].rearrange("j (p t) -> j t p", t=4)
+            for u in range(2):
+                ts = slice(2 * u, 2 * u + 2)
+                nc.vector.tensor_tensor(d[:, ts, :], a_v[:, ts, :], b_sb[jt][:, ts, :], ALU.subtract)
+                for t in range(2 * u, 2 * u + 2):
+                    nc.tensor.transpose(tr[:, t, :], d[:, t, :], ident[:])
             h = sb.tile([P, P, 4], BF16, name=f"hid{jt}", align_bytes=64)
             nc.scalar.activation(h[:], tr[:].rearrange("p t j -> p j t"), ACT.Abs)
             hid.append(h)

@@ -66,6 +66,11 @@ def tile_list_outcomegatedgroups_noted_kernel(
         nc.vector.memset(w_sc[0:HALF], 0)
         nc.vector.memset(wbc_sc[0:HALF], 0)
 
+        warm_in = sb.tile([P, 1], F32, name="warm_in")
+        warm_out = sb.tile([P, 1], F32, name="warm_out")
+        nc.vector.memset(warm_in[:], 0.0)
+        nc.scalar.activation(warm_out[:], warm_in[:], ACT.Sigmoid)
+
         def load_vec(src, name):
             t = sb.tile([P, 2], F32, name=name)
             with nc.allow_non_contiguous_dma(reason="one value a partition and half"):

@@ -20,7 +20,10 @@ ALU = mybir.AluOpType
 
 P = 128
 HALF = 64
-W2_ROW = 4
+QUAD = 32
+PACK = 4
+LIST_COLS = P // 16
+SHIFTED_ROW = 4
 
 
 def tile_list_outcomegatedgroups_noted_kernel(
@@ -34,183 +37,188 @@ def tile_list_outcomegatedgroups_noted_kernel(
         ps = ctx.enter_context(tc.psum_pool(name="ps", bufs=1))
 
         def load_list(src, name):
-            t = sb.tile(list(src.shape), U16, name=name)
-            nc.sync.dma_start(t[:], src)
-            return t
+            tile = sb.tile(list(src.shape), U16, name=name)
+            nc.sync.dma_start(tile[:], src)
+            return tile
 
         def load_words(src, name):
             flat = src[0]
             if len(flat.shape) == 3:
                 flat = flat.rearrange("p n t -> p (n t)")
-            t = sb.tile([P, flat.shape[1]], U8, name=name, align_bytes=64)
-            nc.sync.dma_start(t[:].bitcast(I32), flat.bitcast(I32))
-            return t
+            tile = sb.tile([P, flat.shape[1]], U8, name=name, align_bytes=64)
+            nc.sync.dma_start(tile[:].bitcast(I32), flat.bitcast(I32))
+            return tile
 
-        def load_scale_rows(queue, src, stage, base, col0):
-            rows = src[0].bitcast(I32).rearrange("(s q r) n -> q r s n", s=2, q=2)
-            width = rows.shape[3]
-            for q in range(2):
-                p0 = base + 32 * q
-                queue.dma_start(stage[p0 : p0 + 4, :, col0 : col0 + width], rows[q])
+        def load_scale_rows(src, stage, first):
+            rows = src[0].bitcast(I32).rearrange("(s u i) n -> u i s n", s=2, u=2)
+            for u in range(2):
+                start = first + QUAD * u
+                nc.sync.dma_start(stage[start : start + PACK], rows[u])
 
-        xo_stage = sb.tile([P, 2, T // 4], I32, name="xo_stage", align_bytes=64)
-        xt_stage = sb.tile([P, 2, T // 4], I32, name="xt_stage", align_bytes=64)
-        w2_sc = sb.tile([P, 2, R // 4], I32, name="w2_sc", align_bytes=64)
-        w0_sc = sb.tile([P, 2, R // 4], I32, name="w0_sc", align_bytes=64)
-        w_sc = sb.tile([P, 2, R // 4], I32, name="w_sc", align_bytes=64)
-        wbc_sc = sb.tile([P, 2, 2 * N // 4], I32, name="wbc_sc", align_bytes=64)
+        def load_per_feature(src, name):
+            tile = sb.tile([P, 2], F32, name=name)
+            with nc.allow_non_contiguous_dma(reason="one value a partition and half"):
+                nc.sync.dma_start(tile[:], src.rearrange("(h p) o -> p (h o)", p=P))
+            return tile
+
+        xo_stage = sb.tile([P, 2, T // PACK], I32, name="xo_stage", align_bytes=64)
+        xt_stage = sb.tile([P, 2, T // PACK], I32, name="xt_stage", align_bytes=64)
+        w2_stage = sb.tile([P, 2, R // PACK], I32, name="w2_stage", align_bytes=64)
+        w0_stage = sb.tile([P, 2, R // PACK], I32, name="w0_stage", align_bytes=64)
+        w_rows = sb.tile([P, R // PACK], I32, name="w_rows", align_bytes=64)
+        wb_stage = sb.tile([P, 2, N // PACK], I32, name="wb_stage", align_bytes=64)
+        wc_stage = sb.tile([P, 2, N // PACK], I32, name="wc_stage", align_bytes=64)
         nc.gpsimd.memset(xo_stage[0:HALF], 0)
-        nc.vector.memset(w0_sc[HALF:P], 0)
-        nc.vector.memset(w2_sc[0:HALF], 0)
+        nc.vector.memset(w0_stage[HALF:P], 0)
+        nc.vector.memset(w2_stage[0:HALF], 0)
         nc.gpsimd.memset(xt_stage[HALF:P], 0)
-        nc.vector.memset(w_sc[0:HALF], 0)
-        nc.vector.memset(wbc_sc[0:HALF], 0)
+        nc.vector.memset(w_rows[:], 0)
+        nc.vector.memset(wb_stage[0:HALF], 0)
+        nc.vector.memset(wc_stage[0:HALF], 0)
 
         warm_in = sb.tile([P, 1], F32, name="warm_in")
         warm_out = sb.tile([P, 1], F32, name="warm_out")
         nc.vector.memset(warm_in[:], 0.0)
         nc.scalar.activation(warm_out[:], warm_in[:], ACT.Sigmoid)
 
-        def load_vec(src, name):
-            t = sb.tile([P, 2], F32, name=name)
-            with nc.allow_non_contiguous_dma(reason="one value a partition and half"):
-                nc.sync.dma_start(t[:], src.rearrange("(h p) o -> p (h o)", p=P))
-            return t
-
-        l2 = load_list(offs2, "l2")
-        l1 = load_list(offs, "l1")
-        load_scale_rows(nc.sync, xo_scales, xo_stage, 0, 0)
-        load_scale_rows(nc.sync, w0_scales, w0_sc, HALF, 0)
+        idx2 = load_list(offs2, "idx2")
+        idx = load_list(offs, "idx")
+        load_scale_rows(xo_scales, xo_stage, 0)
+        load_scale_rows(w0_scales, w0_stage, HALF)
         xo_w = load_words(xo_words, "xo_w")
         w0_w = load_words(w0_words, "w0_w")
-        load_scale_rows(nc.sync, w2_scales, w2_sc, W2_ROW, 0)
+        load_scale_rows(w2_scales, w2_stage, SHIFTED_ROW)
+        load_scale_rows(xt_scales, xt_stage, HALF)
         w2_w = load_words(w2_words, "w2_w")
-        load_scale_rows(nc.sync, xt_scales, xt_stage, HALF, 0)
         xt_w = load_words(xt_words, "xt_w")
-        load_scale_rows(nc.sync, w_scales, w_sc, 0, 0)
         w_w = load_words(w_words, "w_w")
-        load_scale_rows(nc.sync, wb_scales, wbc_sc, 0, 0)
-        load_scale_rows(nc.sync, wc_scales, wbc_sc, 0, N // 4)
+        w_src = w_scales[0].bitcast(I32)
+        for quad in range(P // QUAD):
+            nc.sync.dma_start(w_rows[QUAD * quad : QUAD * quad + PACK], w_src[PACK * quad : PACK * (quad + 1)])
+        load_scale_rows(wb_scales, wb_stage, 0)
+        load_scale_rows(wc_scales, wc_stage, SHIFTED_ROW)
         wb_w = load_words(wb_words, "wb_w")
         wc_w = load_words(wc_words, "wc_w")
-        l4 = load_list(offs4, "l4")
-        sp_t = load_vec(sp, "sp_t")
-        bo_t = load_vec(bo, "bo_t")
-        l3 = load_list(offs3, "l3")
-        so_t = load_vec(so, "so_t")
-        l5 = load_list(offs5, "l5")
+        idx5 = load_list(offs5, "idx5")
+        idx4 = load_list(offs4, "idx4")
+        sp_t = load_per_feature(sp, "sp_t")
+        bo_t = load_per_feature(bo, "bo_t")
+        idx3 = load_list(offs3, "idx3")
+        so_t = load_per_feature(so, "so_t")
 
         ident = sb.tile([P, P], F32, name="ident")
         make_identity(nc, ident[:])
 
-        def plane_of(sc, base):
-            if base == 0:
-                nc.vector.tensor_copy(sc[HALF:P, 0, :], sc[0:HALF, 1, :])
-                return sc[:, 0, :].bitcast(U8)
-            nc.vector.tensor_copy(sc[0:HALF, 1, :], sc[HALF:P, 0, :])
-            return sc[:, 1, :].bitcast(U8)
+        def weight_plane(stage, staged_low):
+            if staged_low:
+                nc.vector.tensor_copy(stage[HALF:P, 0, :], stage[0:HALF, 1, :])
+                return stage[:, 0, :].bitcast(U8)
+            nc.vector.tensor_copy(stage[0:HALF, 1, :], stage[HALF:P, 0, :])
+            return stage[:, 1, :].bitcast(U8)
 
-        def table_plane(stage, base, name):
+        def table_plane(stage, first, name):
             plane = sb.tile([P, T], U8, name=name, align_bytes=64)
-            pv = plane[:].bitcast(I32)
-            nc.vector.tensor_copy(pv[0:HALF], stage[base : base + HALF, 0, :])
-            nc.vector.tensor_copy(pv[HALF:P], stage[base : base + HALF, 1, :])
+            as_words = plane[:].bitcast(I32)
+            nc.vector.tensor_copy(as_words[0:HALF], stage[first : first + HALF, 0, :])
+            nc.vector.tensor_copy(as_words[HALF:P], stage[first : first + HALF, 1, :])
             return plane
 
-        def gather(words, plane, lst, jt, g, gs):
+        def gather_slot_tile(words, plane, offsets, jt, picked_words, picked_scales):
             js = slice(jt * P, (jt + 1) * P)
-            piece = lst[:, jt * 8 : (jt + 1) * 8]
-            nc.vector.tensor_copy(gs[:, js], plane[:].indirect(piece))
-            nc.vector.tensor_copy(g[:, js], words[:].bitcast(U32).indirect(piece))
+            piece = offsets[:, jt * LIST_COLS : (jt + 1) * LIST_COLS]
+            nc.vector.tensor_copy(picked_scales[:, js], plane[:].indirect(piece))
+            nc.vector.tensor_copy(picked_words[:, js], words[:].bitcast(U32).indirect(piece))
 
-        xo_pl = table_plane(xo_stage, 0, "xo_pl")
-        w0_pl = plane_of(w0_sc, HALF)
+        xo_plane = table_plane(xo_stage, 0, "xo_plane")
+        w0_plane = weight_plane(w0_stage, staged_low=False)
         xo_g = sb.tile([P, J], U32, name="xo_g", align_bytes=64)
         xt_g = sb.tile([P, J], U32, name="xt_g", align_bytes=64)
         xo_gs = sb.tile([P, J], U8, name="xo_gs", align_bytes=64)
         xt_gs = sb.tile([P, J], U8, name="xt_gs", align_bytes=64)
         b_ps = [ps.tile([P, R], F32, name=f"b{jt}", tag=f"bank{jt}") for jt in range(2)]
         a_ps = [ps.tile([P, R], F32, name=f"a{jt}", tag=f"bank{2 + jt}") for jt in range(2)]
-        b_sb = [sb.tile([P, 4, P], F32, name=f"b_sb{jt}") for jt in range(2)]
+        b_sb = [sb.tile([P, PACK, P], F32, name=f"b_sb{jt}") for jt in range(2)]
+
         for jt in range(2):
             js = slice(jt * P, (jt + 1) * P)
-            gather(xo_w, xo_pl, l2, jt, xo_g, xo_gs)
+            gather_slot_tile(xo_w, xo_plane, idx2, jt, xo_g, xo_gs)
             nc.tensor.matmul_mx(
                 a_ps[jt][:], lhsT=xo_g[:, js].bitcast(E4M3), lhsT_scale=xo_gs[:, js],
-                rhs=w0_w[:].bitcast(E2M1), rhs_scale=w0_pl, start=True, stop=False,
+                rhs=w0_w[:].bitcast(E2M1), rhs_scale=w0_plane, start=True, stop=False,
             )
-        w2_pl = plane_of(w2_sc, 0)[W2_ROW:P]
+        w2_plane = weight_plane(w2_stage, staged_low=True)[SHIFTED_ROW:P]
         for jt in range(2):
             js = slice(jt * P, (jt + 1) * P)
             nc.tensor.matmul_mx(
                 b_ps[jt][:], lhsT=xo_g[:, js].bitcast(E4M3), lhsT_scale=xo_gs[:, js],
-                rhs=w2_w[:].bitcast(E4M3), rhs_scale=w2_pl, start=True, stop=True,
+                rhs=w2_w[:].bitcast(E4M3), rhs_scale=w2_plane, start=True, stop=True,
             )
-            nc.scalar.copy(b_sb[jt][:], b_ps[jt][:].rearrange("j (p t) -> j t p", t=4))
-        xt_pl = table_plane(xt_stage, HALF, "xt_pl")
-        w_pl = plane_of(w_sc, 0)
+            nc.scalar.copy(b_sb[jt][:], b_ps[jt][:].rearrange("j (p t) -> j t p", t=PACK))
+        xt_plane = table_plane(xt_stage, HALF, "xt_plane")
+        w_plane = w_rows[:].bitcast(U8)
         for jt in range(2):
             js = slice(jt * P, (jt + 1) * P)
-            gather(xt_w, xt_pl, l1, jt, xt_g, xt_gs)
+            gather_slot_tile(xt_w, xt_plane, idx, jt, xt_g, xt_gs)
             nc.tensor.matmul_mx(
                 a_ps[jt][:], lhsT=xt_g[:, js].bitcast(E5M2), lhsT_scale=xt_gs[:, js],
-                rhs=w_w[:].bitcast(E2M1), rhs_scale=w_pl, start=False, stop=True,
+                rhs=w_w[:].bitcast(E2M1), rhs_scale=w_plane, start=False, stop=True,
             )
-        wbc_pl = plane_of(wbc_sc, 0)
+        wb_plane = weight_plane(wb_stage, staged_low=True)
+        wc_plane = weight_plane(wc_stage, staged_low=True)[SHIFTED_ROW:P]
 
         hid = []
         for jt in range(2):
-            d = sb.tile([P, 4, P], F32, name=f"d{jt}")
-            tr = ps.tile([P, 4, P], F32, name=f"tr{jt}", tag=f"bank{4 + jt}")
-            a_v = a_ps[jt][:].rearrange("j (p t) -> j t p", t=4)
-            for u in range(2):
-                ts = slice(2 * u, 2 * u + 2)
-                nc.vector.tensor_tensor(d[:, ts, :], a_v[:, ts, :], b_sb[jt][:, ts, :], ALU.subtract)
-                for t in range(2 * u, 2 * u + 2):
-                    nc.tensor.transpose(tr[:, t, :], d[:, t, :], ident[:])
-            h = sb.tile([P, P, 4], BF16, name=f"hid{jt}", align_bytes=64)
-            nc.scalar.activation(h[:], tr[:].rearrange("p t j -> p j t"), ACT.Abs)
-            hid.append(h)
+            diff = sb.tile([P, PACK, P], F32, name=f"diff{jt}")
+            turned = ps.tile([P, PACK, P], F32, name=f"turned{jt}", tag=f"bank{4 + jt}")
+            a_by_t = a_ps[jt][:].rearrange("j (p t) -> j t p", t=PACK)
+            for t in range(PACK):
+                nc.vector.tensor_tensor(diff[:, t, :], a_by_t[:, t, :], b_sb[jt][:, t, :], ALU.subtract)
+                nc.tensor.transpose(turned[:, t, :], diff[:, t, :], ident[:])
+            rounded = sb.tile([P, P, PACK], BF16, name=f"hid{jt}", align_bytes=64)
+            nc.scalar.activation(rounded[:], turned[:].rearrange("p t j -> p j t"), ACT.Abs)
+            hid.append(rounded)
 
         p_sb = [sb.tile([P, J], F32, name=f"p_sb{h}") for h in range(2)]
         q_sb = sb.tile([P, 2, J], F32, name="q_sb")
+        p_banks = ((0, 1), (6, 7))
         for jt in range(2):
             js = slice(jt * P, (jt + 1) * P)
             codes = sb.tile([P, P], U32, name=f"codes{jt}", align_bytes=64)
-            hsc = sb.tile([P, P], U8, name=f"hsc{jt}", align_bytes=64)
+            hid_plane = sb.tile([P, P], U8, name=f"hid_plane{jt}", align_bytes=64)
             nc.vector.quantize_mx(
-                out=codes[:].bitcast(E4M3), scales=hsc[:], in_=hid[jt][:].rearrange("p j t -> p (j t)")
+                out=codes[:].bitcast(E4M3), scales=hid_plane[:], in_=hid[jt][:].rearrange("p j t -> p (j t)")
             )
-            p_ps = [ps.tile([P, P], F32, name=f"p{jt}{h}", tag=f"bank{(0, 1, 6, 7)[2 * jt + h]}") for h in range(2)]
+            p_ps = [ps.tile([P, P], F32, name=f"p{jt}{h}", tag=f"bank{p_banks[jt][h]}") for h in range(2)]
             q_ps = ps.tile([P, 2, P], F32, name=f"q{jt}", tag=f"bank{2 + jt}")
-            for h in range(2):
-                nc.tensor.matmul_mx(
-                    p_ps[h][:], lhsT=wb_w[:, 2 * P * h : 2 * P * (h + 1)].bitcast(E2M1),
-                    lhsT_scale=wbc_pl[:, P * h : P * (h + 1)],
-                    rhs=codes[:].bitcast(E4M3), rhs_scale=hsc[:], start=True, stop=True,
-                )
-            for h in range(2):
-                nc.tensor.matmul_mx(
-                    q_ps[:, h, :], lhsT=wc_w[:, 4 * P * h : 4 * P * (h + 1)].bitcast(E4M3),
-                    lhsT_scale=wbc_pl[:, N + P * h : N + P * (h + 1)],
-                    rhs=codes[:].bitcast(E4M3), rhs_scale=hsc[:], start=True, stop=True,
-                )
-            nc.scalar.copy(p_sb[0][:, js], p_ps[0][:])
-            nc.vector.tensor_copy(p_sb[1][:, js], p_ps[1][:])
-            nc.vector.tensor_copy(q_sb[:, :, js], q_ps[:])
 
+            def outcome(dst, words, fmt, word_bytes, plane, h):
+                nc.tensor.matmul_mx(
+                    dst, lhsT=words[:, word_bytes * P * h : word_bytes * P * (h + 1)].bitcast(fmt),
+                    lhsT_scale=plane[:, P * h : P * (h + 1)],
+                    rhs=codes[:].bitcast(E4M3), rhs_scale=hid_plane[:], start=True, stop=True,
+                )
+
+            outcome(p_ps[0][:], wb_w, E2M1, 2, wb_plane, 0)
+            nc.scalar.copy(p_sb[0][:, js], p_ps[0][:])
+            for h in range(2):
+                outcome(q_ps[:, h, :], wc_w, E4M3, 4, wc_plane, h)
+            nc.vector.tensor_copy(q_sb[:, :, js], q_ps[:])
+            outcome(p_ps[1][:], wb_w, E2M1, 2, wb_plane, 1)
+            nc.vector.tensor_copy(p_sb[1][:, js], p_ps[1][:])
+
+        q_picked = sb.tile([P, 2, O], F32, name="q_picked")
+        for h in range(2):
+            nc.vector.tensor_copy(q_picked[:, h, :], q_sb[:, h, :].indirect(idx5[:]))
         for h in range(2):
             gate = sb.tile([P, O], F32, name=f"gate{h}")
-            val = sb.tile([P, O], F32, name=f"val{h}")
-            qg = sb.tile([P, O], F32, name=f"qg{h}")
-            prod = sb.tile([P, O], F32, name=f"prod{h}")
-            res = sb.tile([P, O], F32, name=f"res{h}")
+            weighted = sb.tile([P, O], F32, name=f"weighted{h}")
+            product = sb.tile([P, O], F32, name=f"product{h}")
+            result = sb.tile([P, O], F32, name=f"result{h}")
             nc.scalar.activation(
-                gate[:], p_sb[h][:].indirect(l4[:]), ACT.Sigmoid,
+                gate[:], p_sb[h][:].indirect(idx4[:]), ACT.Sigmoid,
                 bias=bo_t[:, h : h + 1], scale=sp_t[:, h : h + 1],
             )
-            nc.scalar.activation(val[:], p_sb[h][:].indirect(l3[:]), ACT.Copy, scale=so_t[:, h : h + 1])
-            nc.vector.tensor_copy(qg[:], q_sb[:, h, :].indirect(l5[:]))
-            nc.vector.tensor_tensor(prod[:], val[:], gate[:], ALU.mult)
-            nc.vector.tensor_tensor(res[:], prod[:], qg[:], ALU.subtract)
-            nc.sync.dma_start(out[h * P : (h + 1) * P, :], res[:])
+            nc.scalar.activation(weighted[:], p_sb[h][:].indirect(idx3[:]), ACT.Copy, scale=so_t[:, h : h + 1])
+            nc.vector.tensor_tensor(product[:], weighted[:], gate[:], ALU.mult)
+            nc.vector.tensor_tensor(result[:], product[:], q_picked[:, h, :], ALU.subtract)
+            nc.sync.dma_start(out[h * P : (h + 1) * P, :], result[:])

from contextlib import ExitStack

import concourse.mybir as mybir
from concourse.masks import make_identity

K, T, J, R, N, O = 512, 1024, 256, 512, 256, 128
FLOPS = 3 * 2 * K * R * J + 2 * 2 * R * N * J

F32 = mybir.dt.float32
BF16 = mybir.dt.bfloat16
I32 = mybir.dt.int32
U32 = mybir.dt.uint32
U16 = mybir.dt.uint16
U8 = mybir.dt.uint8
E4M3 = mybir.dt.float8_e4m3fn_x4
E5M2 = mybir.dt.float8_e5m2_x4
E2M1 = mybir.dt.float4_e2m1fn_x4
ACT = mybir.ActivationFunctionType
ALU = mybir.AluOpType

P = 128
HALF = 64
QUAD = 32
PACK = 4
LIST_COLS = P // 16
SHIFTED_ROW = 4


def tile_list_outcomegatedgroups_noted_kernel(
    tc, xt_words, xt_scales, xo_words, xo_scales, w_words, w_scales, w0_words, w0_scales,
    w2_words, w2_scales, wb_words, wb_scales, wc_words, wc_scales, so, sp, bo,
    offs, offs2, offs3, offs4, offs5, out,
):
    nc = tc.nc
    with ExitStack() as ctx:
        sb = ctx.enter_context(tc.tile_pool(name="sb", bufs=1))
        ps = ctx.enter_context(tc.psum_pool(name="ps", bufs=1))

        def load_list(src, name):
            tile = sb.tile(list(src.shape), U16, name=name)
            nc.sync.dma_start(tile[:], src)
            return tile

        def load_words(src, name):
            flat = src[0]
            if len(flat.shape) == 3:
                flat = flat.rearrange("p n t -> p (n t)")
            tile = sb.tile([P, flat.shape[1]], U8, name=name, align_bytes=64)
            nc.sync.dma_start(tile[:].bitcast(I32), flat.bitcast(I32))
            return tile

        def load_scale_rows(src, stage, first):
            rows = src[0].bitcast(I32).rearrange("(s u i) n -> u i s n", s=2, u=2)
            for u in range(2):
                start = first + QUAD * u
                nc.sync.dma_start(stage[start : start + PACK], rows[u])

        def load_per_feature(src, name):
            tile = sb.tile([P, 2], F32, name=name)
            with nc.allow_non_contiguous_dma(reason="one value a partition and half"):
                nc.sync.dma_start(tile[:], src.rearrange("(h p) o -> p (h o)", p=P))
            return tile

        xo_stage = sb.tile([P, 2, T // PACK], I32, name="xo_stage", align_bytes=64)
        xt_stage = sb.tile([P, 2, T // PACK], I32, name="xt_stage", align_bytes=64)
        w2_stage = sb.tile([P, 2, R // PACK], I32, name="w2_stage", align_bytes=64)
        w0_stage = sb.tile([P, 2, R // PACK], I32, name="w0_stage", align_bytes=64)
        w_rows = sb.tile([P, R // PACK], I32, name="w_rows", align_bytes=64)
        wb_stage = sb.tile([P, 2, N // PACK], I32, name="wb_stage", align_bytes=64)
        wc_stage = sb.tile([P, 2, N // PACK], I32, name="wc_stage", align_bytes=64)
        nc.gpsimd.memset(xo_stage[0:HALF], 0)
        nc.vector.memset(w0_stage[HALF:P], 0)
        nc.vector.memset(w2_stage[0:HALF], 0)
        nc.gpsimd.memset(xt_stage[HALF:P], 0)
        nc.vector.memset(w_rows[:], 0)
        nc.vector.memset(wb_stage[0:HALF], 0)
        nc.vector.memset(wc_stage[0:HALF], 0)

        warm_in = sb.tile([P, 1], F32, name="warm_in")
        warm_out = sb.tile([P, 1], F32, name="warm_out")
        nc.vector.memset(warm_in[:], 0.0)
        nc.scalar.activation(warm_out[:], warm_in[:], ACT.Sigmoid)

        idx2 = load_list(offs2, "idx2")
        idx = load_list(offs, "idx")
        load_scale_rows(xo_scales, xo_stage, 0)
        load_scale_rows(w0_scales, w0_stage, HALF)
        xo_w = load_words(xo_words, "xo_w")
        w0_w = load_words(w0_words, "w0_w")
        load_scale_rows(w2_scales, w2_stage, SHIFTED_ROW)
        load_scale_rows(xt_scales, xt_stage, HALF)
        w2_w = load_words(w2_words, "w2_w")
        xt_w = load_words(xt_words, "xt_w")
        w_w = load_words(w_words, "w_w")
        w_src = w_scales[0].bitcast(I32)
        for quad in range(P // QUAD):
            nc.sync.dma_start(w_rows[QUAD * quad : QUAD * quad + PACK], w_src[PACK * quad : PACK * (quad + 1)])
        load_scale_rows(wb_scales, wb_stage, 0)
        load_scale_rows(wc_scales, wc_stage, SHIFTED_ROW)
        wb_w = load_words(wb_words, "wb_w")
        wc_w = load_words(wc_words, "wc_w")
        idx5 = load_list(offs5, "idx5")
        idx4 = load_list(offs4, "idx4")
        sp_t = load_per_feature(sp, "sp_t")
        bo_t = load_per_feature(bo, "bo_t")
        idx3 = load_list(offs3, "idx3")
        so_t = load_per_feature(so, "so_t")

        ident = sb.tile([P, P], F32, name="ident")
        make_identity(nc, ident[:])

        def weight_plane(stage, staged_low):
            if staged_low:
                nc.vector.tensor_copy(stage[HALF:P, 0, :], stage[0:HALF, 1, :])
                return stage[:, 0, :].bitcast(U8)
            nc.vector.tensor_copy(stage[0:HALF, 1, :], stage[HALF:P, 0, :])
            return stage[:, 1, :].bitcast(U8)

        def table_plane(stage, first, name):
            plane = sb.tile([P, T], U8, name=name, align_bytes=64)
            as_words = plane[:].bitcast(I32)
            nc.vector.tensor_copy(as_words[0:HALF], stage[first : first + HALF, 0, :])
            nc.vector.tensor_copy(as_words[HALF:P], stage[first : first + HALF, 1, :])
            return plane

        def gather_slot_tile(words, plane, offsets, jt, picked_words, picked_scales):
            js = slice(jt * P, (jt + 1) * P)
            piece = offsets[:, jt * LIST_COLS : (jt + 1) * LIST_COLS]
            nc.vector.tensor_copy(picked_scales[:, js], plane[:].indirect(piece))
            nc.vector.tensor_copy(picked_words[:, js], words[:].bitcast(U32).indirect(piece))

        xo_plane = table_plane(xo_stage, 0, "xo_plane")
        w0_plane = weight_plane(w0_stage, staged_low=False)
        xo_g = sb.tile([P, J], U32, name="xo_g", align_bytes=64)
        xt_g = sb.tile([P, J], U32, name="xt_g", align_bytes=64)
        xo_gs = sb.tile([P, J], U8, name="xo_gs", align_bytes=64)
        xt_gs = sb.tile([P, J], U8, name="xt_gs", align_bytes=64)
        b_ps = [ps.tile([P, R], F32, name=f"b{jt}", tag=f"bank{jt}") for jt in range(2)]
        a_ps = [ps.tile([P, R], F32, name=f"a{jt}", tag=f"bank{2 + jt}") for jt in range(2)]
        b_sb = [sb.tile([P, PACK, P], F32, name=f"b_sb{jt}") for jt in range(2)]

        for jt in range(2):
            js = slice(jt * P, (jt + 1) * P)
            gather_slot_tile(xo_w, xo_plane, idx2, jt, xo_g, xo_gs)
            nc.tensor.matmul_mx(
                a_ps[jt][:], lhsT=xo_g[:, js].bitcast(E4M3), lhsT_scale=xo_gs[:, js],
                rhs=w0_w[:].bitcast(E2M1), rhs_scale=w0_plane, start=True, stop=False,
            )
        w2_plane = weight_plane(w2_stage, staged_low=True)[SHIFTED_ROW:P]
        for jt in range(2):
            js = slice(jt * P, (jt + 1) * P)
            nc.tensor.matmul_mx(
                b_ps[jt][:], lhsT=xo_g[:, js].bitcast(E4M3), lhsT_scale=xo_gs[:, js],
                rhs=w2_w[:].bitcast(E4M3), rhs_scale=w2_plane, start=True, stop=True,
            )
            nc.scalar.copy(b_sb[jt][:], b_ps[jt][:].rearrange("j (p t) -> j t p", t=PACK))
        xt_plane = table_plane(xt_stage, HALF, "xt_plane")
        w_plane = w_rows[:].bitcast(U8)
        for jt in range(2):
            js = slice(jt * P, (jt + 1) * P)
            gather_slot_tile(xt_w, xt_plane, idx, jt, xt_g, xt_gs)
            nc.tensor.matmul_mx(
                a_ps[jt][:], lhsT=xt_g[:, js].bitcast(E5M2), lhsT_scale=xt_gs[:, js],
                rhs=w_w[:].bitcast(E2M1), rhs_scale=w_plane, start=False, stop=True,
            )
        wb_plane = weight_plane(wb_stage, staged_low=True)
        wc_plane = weight_plane(wc_stage, staged_low=True)[SHIFTED_ROW:P]

        hid = []
        for jt in range(2):
            diff = sb.tile([P, PACK, P], F32, name=f"diff{jt}")
            turned = ps.tile([P, PACK, P], F32, name=f"turned{jt}", tag=f"bank{4 + jt}")
            a_by_t = a_ps[jt][:].rearrange("j (p t) -> j t p", t=PACK)
            for t in range(PACK):
                nc.vector.tensor_tensor(diff[:, t, :], a_by_t[:, t, :], b_sb[jt][:, t, :], ALU.subtract)
                nc.tensor.transpose(turned[:, t, :], diff[:, t, :], ident[:])
            rounded = sb.tile([P, P, PACK], BF16, name=f"hid{jt}", align_bytes=64)
            nc.scalar.activation(rounded[:], turned[:].rearrange("p t j -> p j t"), ACT.Abs)
            hid.append(rounded)

        p_sb = [sb.tile([P, J], F32, name=f"p_sb{h}") for h in range(2)]
        q_sb = sb.tile([P, 2, J], F32, name="q_sb")
        p_banks = ((0, 1), (6, 7))
        for jt in range(2):
            js = slice(jt * P, (jt + 1) * P)
            codes = sb.tile([P, P], U32, name=f"codes{jt}", align_bytes=64)
            hid_plane = sb.tile([P, P], U8, name=f"hid_plane{jt}", align_bytes=64)
            nc.vector.quantize_mx(
                out=codes[:].bitcast(E4M3), scales=hid_plane[:], in_=hid[jt][:].rearrange("p j t -> p (j t)")
            )
            p_ps = [ps.tile([P, P], F32, name=f"p{jt}{h}", tag=f"bank{p_banks[jt][h]}") for h in range(2)]
            q_ps = ps.tile([P, 2, P], F32, name=f"q{jt}", tag=f"bank{2 + jt}")

            def outcome(dst, words, fmt, word_bytes, plane, h):
                nc.tensor.matmul_mx(
                    dst, lhsT=words[:, word_bytes * P * h : word_bytes * P * (h + 1)].bitcast(fmt),
                    lhsT_scale=plane[:, P * h : P * (h + 1)],
                    rhs=codes[:].bitcast(E4M3), rhs_scale=hid_plane[:], start=True, stop=True,
                )

            outcome(p_ps[0][:], wb_w, E2M1, 2, wb_plane, 0)
            nc.scalar.copy(p_sb[0][:, js], p_ps[0][:])
            for h in range(2):
                outcome(q_ps[:, h, :], wc_w, E4M3, 4, wc_plane, h)
            nc.vector.tensor_copy(q_sb[:, :, js], q_ps[:])
            outcome(p_ps[1][:], wb_w, E2M1, 2, wb_plane, 1)
            nc.vector.tensor_copy(p_sb[1][:, js], p_ps[1][:])

        q_picked = sb.tile([P, 2, O], F32, name="q_picked")
        for h in range(2):
            nc.vector.tensor_copy(q_picked[:, h, :], q_sb[:, h, :].indirect(idx5[:]))
        for h in range(2):
            gate = sb.tile([P, O], F32, name=f"gate{h}")
            weighted = sb.tile([P, O], F32, name=f"weighted{h}")
            product = sb.tile([P, O], F32, name=f"product{h}")
            result = sb.tile([P, O], F32, name=f"result{h}")
            nc.scalar.activation(
                gate[:], p_sb[h][:].indirect(idx4[:]), ACT.Sigmoid,
                bias=bo_t[:, h : h + 1], scale=sp_t[:, h : h + 1],
            )
            nc.scalar.activation(weighted[:], p_sb[h][:].indirect(idx3[:]), ACT.Copy, scale=so_t[:, h : h + 1])
            nc.vector.tensor_tensor(product[:], weighted[:], gate[:], ALU.mult)
            nc.vector.tensor_tensor(result[:], product[:], q_picked[:, h, :], ALU.subtract)
            nc.sync.dma_start(out[h * P : (h + 1) * P, :], result[:])
